import numpy as np
import ml_dtypes


def mxq(x, axis, fmt="e4m3"):
    dtype, down = {"e4m3": (ml_dtypes.float8_e4m3fn, 7), "e5m2": (ml_dtypes.float8_e5m2, 14)}[fmt]
    v = np.moveaxis(np.asarray(x, np.float32).astype(ml_dtypes.bfloat16).astype(np.float64), axis, -1)
    blocks = v.reshape(v.shape[:-1] + (-1, 32))
    amax = np.abs(blocks).max(-1, keepdims=True)
    byte = np.maximum(np.where(amax > 0, np.frexp(amax)[1] - 1 + 127, 0) - down, 1)
    scale = np.exp2(byte - 127.0)
    codes = (blocks / scale).astype(np.float32).astype(dtype).astype(np.float64)
    return np.moveaxis((codes * scale).reshape(v.shape), -1, axis)


WIDE = False


def mx_kscale(k):
    if not WIDE:
        return np.ones(k)
    levels = np.array([10, -10, 5, -5, 0])
    if k % 512:
        return np.exp2(np.random.permutation(np.resize(levels, k // 32))).repeat(32)
    a = np.empty((k // 512, 16))
    for p in range(k // 512):
        a[p, :8] = np.random.permutation(np.resize(levels, 8))
        for g in range(8):
            far = levels[np.abs(levels - a[p, g]) >= 10]
            a[p, g + 8] = far[np.random.randint(len(far))]
    return np.exp2(a.ravel()).repeat(32)


BF16 = ml_dtypes.bfloat16


def bf(x):
    return np.asarray(x, np.float32).astype(BF16)


def f64(x):
    return np.asarray(x).astype(np.float64)


E2M1 = np.array([0.0, 0.5, 1.0, 1.5, 2.0, 3.0, 4.0, 6.0, -0.0, -0.5, -1.0, -1.5, -2.0, -3.0, -4.0, -6.0])


def pack_weight(w, fmt):
    k, n = w.shape
    w = f64(bf(w)).reshape(k // 32, 32, n)
    amax = np.abs(w).max(1)
    if fmt == "e4m3":
        byte = np.frexp(amax)[1] - 1 + 127 - 7
    else:
        mant, ex = np.frexp(amax / 6.0)
        byte = np.where(mant > 0.5, ex, ex - 1) + 127
    byte = np.clip(np.where(amax > 0, byte, 1), 1, 254)
    scaled = (w * np.exp2(127.0 - byte)[:, None, :]).reshape(k, n).astype(np.float32)
    by_word = np.ascontiguousarray(scaled.reshape(k // 512, 128, 4, n).transpose(0, 1, 3, 2))
    if fmt == "e4m3":
        words = by_word.astype(ml_dtypes.float8_e4m3fn).view(np.uint8)
    else:
        c = by_word.astype(ml_dtypes.float4_e2m1fn).view(np.uint8) & 0xF
        words = c[..., 0::2] | (c[..., 1::2] << 4)
    return np.ascontiguousarray(words), np.ascontiguousarray(byte.astype(np.uint8).reshape(k // 512, 16, n))


def unpack_weight(words, scales, fmt):
    g, p, n, _ = words.shape
    if fmt == "e4m3":
        vals = np.ascontiguousarray(words).view(ml_dtypes.float8_e4m3fn).astype(np.float64)
    else:
        nib = np.empty((g, p, n, 4), np.uint8)
        nib[..., 0::2] = words & 0xF
        nib[..., 1::2] = words >> 4
        vals = E2M1[nib]
    vals = vals * np.repeat(np.exp2(scales.astype(np.float64) - 127.0), 8, axis=1)[..., None]
    return vals.transpose(0, 1, 3, 2).reshape(g * 512, n)
def pack4(w):
    words, scales = pack_weight(w, "e2m1")
    return words.reshape(words.shape[0], 128, -1), scales


def unpack4(words, scales):
    return unpack_weight(words.reshape(words.shape[0], 128, -1, 2), scales, "e2m1")


M, K, N, R = 1024, 1024, 512, 4


def setup_inputs():
    s = mx_kscale(K)
    x = np.random.standard_normal((M, K)) * s
    u = np.random.standard_normal((K, R * N)) / np.sqrt(K) / s[:, None]
    v = np.random.standard_normal((K, R * N)) / np.sqrt(K * R) / s[:, None]
    lin = np.random.standard_normal((K, N)) / np.sqrt(K) / s[:, None]
    u_words, u_scales = pack4(u)
    v_words, v_scales = pack_weight(v, "e4m3")
    return {"x": bf(x),
            "u_words": u_words, "u_scales": u_scales,
            "v_words": v_words, "v_scales": v_scales,
            "lin": bf(lin),
            "bias": bf(0.3 * np.random.standard_normal(N))}


def reference(x, u_words, u_scales, v_words, v_scales, lin, bias):
    xq = mxq(f64(x), 1, "e4m3")
    a = xq @ unpack4(u_words, u_scales)
    c = xq @ unpack_weight(v_words, v_scales, "e4m3")
    linear = xq @ mxq(f64(lin), 0, "e4m3")
    quadratic = (a * c).reshape(M, R, N).sum(axis=1)
    return quadratic + linear + f64(bias)

@@ -1,0 +1,258 @@
+from contextlib import ExitStack
+
+import concourse.mybir as mybir
+from concourse.masks import make_identity
+
+M, K, N, R = 1024, 1024, 512, 4
+FLOPS = 2 * M * K * (2 * R * N + N) + 2 * M * R * N + M * N
+
+F32 = mybir.dt.float32
+BF16 = mybir.dt.bfloat16
+I32 = mybir.dt.int32
+U32 = mybir.dt.uint32
+U8 = mybir.dt.uint8
+FP8X4 = mybir.dt.float8_e4m3fn_x4
+FP4X4 = mybir.dt.float4_e2m1fn_x4
+ADD = mybir.AluOpType.add
+MULT = mybir.AluOpType.mult
+
+P = 128
+PACK = 4
+K_PASS = P * PACK
+G = K // K_PASS
+MT = M // P
+V_ROW = 4
+WARMUP = 4
+LIN_PIECE = 128
+
+
+def tile_volterra_quadratic_equaliser_s10_kernel(tc, x, u_words, u_scales, v_words, v_scales, lin, bias, out):
+    nc = tc.nc
+
+    with ExitStack() as ctx:
+        keep = ctx.enter_context(tc.tile_pool(name="keep", bufs=1))
+        stage = ctx.enter_context(tc.tile_pool(name="stage", bufs=4))
+        psum = ctx.enter_context(tc.psum_pool(name="psum", bufs=8))
+        ctx.enter_context(tc.manual_schedule())
+
+        def kept(shape, dtype, name):
+            return keep.tile(shape, dtype, name=name, align_bytes=256)
+
+        def new_bank():
+            return psum.tile([P, N], F32, name="bank", tag="bank")
+
+        ones = kept([P, N], BF16, "ones")
+        bias_row = kept([P, N], BF16, "bias_row")
+        bias_all = kept([P, N], F32, "bias_all")
+        ident = kept([P, P], F32, "ident")
+        u_plane = kept([P, G, R * N], U8, "u_plane")
+        v_plane = kept([P, G, R * N], U8, "v_plane")
+        x_raw = [kept([P, K], BF16, "x_raw%d" % m) for m in range(2)]
+        x_pair = [kept([P, 2, K], BF16, "x_pair%d" % j) for j in range(3)]
+        x_codes = [kept([P, G * P], U32, "x_codes%d" % m) for m in range(MT)]
+        x_plane = [kept([P, G * P], U8, "x_plane%d" % m) for m in range(MT)]
+        u_codes = [kept([P, G, 2 * N], U8, "u_codes%d" % e) for e in range(R)]
+        v_codes = [kept([P, G, N], U32, "v_codes%d" % e) for e in range(R)]
+        lin_raw = [kept([P, PACK, N], BF16, "lin_raw%d" % g) for g in range(G)]
+        lin_grouped = [kept([P, N, PACK], BF16, "lin_grouped%d" % g) for g in range(G)]
+        lin_codes = [kept([P, N], U32, "lin_codes%d" % g) for g in range(G)]
+        lin_plane = [kept([P, N], U8, "lin_plane%d" % g) for g in range(G)]
+        acc = [kept([P, N], F32, "acc%d" % m) for m in range(MT)]
+
+        def x_rows(m):
+            if m < 2:
+                return x_raw[m][:]
+            return x_pair[m // 2 - 1][:, m % 2, :]
+
+        nc.vector.memset(ones[:], 1.0)
+        nc.vector.memset(u_plane[:].rearrange("p g n -> p (g n)").bitcast(I32), 0)
+        nc.vector.memset(v_plane[:].rearrange("p g n -> p (g n)").bitcast(I32), 0)
+        nc.vector.memset(bias_row[:], 0.0)
+        make_identity(nc, ident[:])
+
+        u_src = u_words.rearrange("g p b -> p g b")
+        v_src = v_words.rearrange("g p n t -> p g (n t)")
+        us_src = u_scales.rearrange("g q n -> q g n")
+        vs_src = v_scales.rearrange("g q n -> q g n")
+
+        def load_u(e):
+            nc.sync.dma_start(out=u_codes[e][:].bitcast(I32), in_=u_src[:, :, 2 * N * e : 2 * N * (e + 1)].bitcast(I32))
+
+        def load_v(e):
+            nc.sync.dma_start(out=v_codes[e][:].bitcast(I32), in_=v_src[:, :, 4 * N * e : 4 * N * (e + 1)].bitcast(I32))
+
+        def load_scales(plane, src, row):
+            for q in range(4):
+                nc.sync.dma_start(out=plane[32 * q + row : 32 * q + row + 4, :, :].bitcast(I32), in_=src[4 * q : 4 * q + 4, :, :].bitcast(I32))
+
+        def load_x_pair(j):
+            rows = x[2 * P * (j + 1) : 2 * P * (j + 2), :]
+            nc.sync.dma_start(out=x_pair[j][:], in_=rows.rearrange("(h p) k -> p h k", p=P))
+
+        for m in range(2):
+            nc.sync.dma_start(out=x_raw[m][:], in_=x[P * m : P * (m + 1), :])
+        load_u(0)
+        load_scales(u_plane, us_src, 0)
+        load_v(0)
+        nc.sync.dma_start(out=bias_row[0:1, :], in_=bias.rearrange("(o n) -> o n", o=1))
+        load_x_pair(0)
+        load_scales(v_plane, vs_src, V_ROW)
+        load_x_pair(1)
+        load_x_pair(2)
+        load_u(1)
+        load_v(1)
+        for g in range(G):
+            nc.sync.dma_start(out=lin_raw[g][:], in_=lin[K_PASS * g : K_PASS * (g + 1), :].rearrange("(p j) n -> p j n", j=PACK))
+        for e in range(2, R):
+            load_u(e)
+            load_v(e)
+
+        x_grouped = {}
+
+        def turn_x(m):
+            words = x_rows(m).bitcast(F32)
+            bank = new_bank()
+            for g in range(G):
+                for h in range(2):
+                    col = P * (2 * g + h)
+                    nc.tensor.transpose(bank[:, col : col + P], words[:, 2 * P * g + h : 2 * P * (g + 1) : 2], ident[:])
+            grouped = stage.tile([P, G * P * PACK], BF16, name="x_grouped", align_bytes=256)
+            nc.scalar.copy(
+                out=grouped[:].bitcast(F32).rearrange("p (g r h) -> p g r h", g=G, h=2),
+                in_=bank[:].rearrange("p (g h r) -> p g r h", g=G, h=2),
+            )
+            x_grouped[m] = grouped
+
+        def quantize_x(m):
+            nc.vector.quantize_mx(out=x_codes[m][:].bitcast(FP8X4), scales=x_plane[m][:], in_=x_grouped[m][:])
+
+        def passes(bank_cols, m, rhs_of, scale_of):
+            for g in range(G):
+                nc.tensor.matmul_mx(
+                    out=bank_cols,
+                    lhsT=x_codes[m][:, P * g : P * (g + 1)].bitcast(FP8X4),
+                    lhsT_scale=x_plane[m][:, P * g : P * (g + 1)],
+                    rhs=rhs_of(g),
+                    rhs_scale=scale_of(g),
+                    start=(g == 0),
+                    stop=(g == G - 1),
+                )
+
+        def left(m, e, parts=1):
+            bank = new_bank()
+            passes(bank[:], m, lambda g: u_codes[e][:, g, :].bitcast(FP4X4), lambda g: u_plane[:, g, N * e : N * (e + 1)])
+            a_sb = stage.tile([P, N], F32, name="a_sb")
+            w = N // parts
+            for j in range(parts):
+                nc.scalar.copy(out=a_sb[:, w * j : w * (j + 1)], in_=bank[:, w * j : w * (j + 1)])
+            return a_sb
+
+        def right(m, e, lo=0, hi=N):
+            bank = new_bank()
+            passes(
+                bank[:, 0 : hi - lo],
+                m,
+                lambda g: v_codes[e][:, g, lo:hi].bitcast(FP8X4),
+                lambda g: v_plane[V_ROW:P, g, N * e + lo : N * e + hi],
+            )
+            return bank[:, 0 : hi - lo]
+
+        def multiply(dst, c_bank, a_sb):
+            nc.vector.tensor_tensor(out=dst, in0=c_bank, in1=a_sb, op=MULT)
+
+        def add_into(engine, m, term, lo=0, hi=N):
+            engine.tensor_tensor(out=acc[m][:, lo:hi], in0=acc[m][:, lo:hi], in1=term, op=ADD)
+
+        def group_lin(piece):
+            g, c = divmod(piece, N // LIN_PIECE)
+            cols = slice(LIN_PIECE * c, LIN_PIECE * (c + 1))
+            nc.scalar.copy(
+                out=lin_grouped[g][:, cols, :].rearrange("p (c i) t -> p c t i", i=4),
+                in_=lin_raw[g][:, :, cols].rearrange("p t (c i) -> p c t i", i=4),
+            )
+
+        def quantize_lin(g):
+            nc.vector.quantize_mx(
+                out=lin_codes[g][:].bitcast(FP8X4),
+                scales=lin_plane[g][:],
+                in_=lin_grouped[g][:].rearrange("p n t -> p (n t)"),
+            )
+
+        def store(m, lo=0, hi=N):
+            nc.sync.dma_start(out=out[P * m : P * (m + 1), lo:hi], in_=acc[m][:, lo:hi])
+
+        warm = new_bank()
+        for i in range(WARMUP):
+            nc.tensor.matmul(warm[:], lhsT=ones[:, 0:P], rhs=ones[:], start=True, stop=True)
+
+        turn_x(0)
+        turn_x(1)
+        quantize_x(0)
+        quantize_x(1)
+        bias_bank = new_bank()
+        nc.tensor.matmul(bias_bank[:], lhsT=ones[:, 0:P], rhs=bias_row[:], start=True, stop=True)
+        a0 = left(0, 0)
+        a1 = left(1, 0)
+        nc.scalar.copy(out=bias_all[:], in_=bias_bank[:])
+        turn_x(2)
+        turn_x(3)
+        quantize_x(2)
+        quantize_x(3)
+        for m, a_sb in ((0, a0), (1, a1)):
+            multiply(acc[m][:], right(m, 0), a_sb[:])
+            add_into(nc.gpsimd, m, bias_all[:])
+        for m in range(2, MT):
+            if m < 4:
+                turn_x(2 * m)
+                turn_x(2 * m + 1)
+            a_sb = left(m, 0)
+            if m < 4:
+                quantize_x(2 * m)
+                quantize_x(2 * m + 1)
+            elif m % 2 == 0:
+                group_lin(m // 2 - 2)
+            multiply(acc[m][:], right(m, 0), a_sb[:])
+            add_into(nc.gpsimd, m, bias_all[:])
+
+        waiting = []
+        for i in range(2 * MT):
+            e, m = 1 + i // MT, i % MT
+            a_sb = left(m, e)
+            if i % 2 == 0 and i // 2 + 2 < G * N // LIN_PIECE:
+                group_lin(i // 2 + 2)
+            prod = stage.tile([P, N], F32, name="prod")
+            multiply(prod[:], right(m, e), a_sb[:])
+            if i % 2 == 0:
+                for wm, wprod in waiting:
+                    add_into(nc.vector, wm, wprod[:])
+                waiting = []
+                add_into(nc.gpsimd, m, prod[:])
+            else:
+                waiting = [(m, prod)]
+            if i == 5:
+                quantize_lin(0)
+            if i == 13:
+                quantize_lin(1)
+
+        e = R - 1
+        for m in range(MT):
+            d_bank = new_bank()
+            passes(d_bank[:], m, lambda g: lin_codes[g][:].bitcast(FP8X4), lambda g: lin_plane[g][:])
+            nc.vector.tensor_tensor(out=acc[m][:], in0=d_bank[:], in1=acc[m][:], op=ADD)
+            prod = stage.tile([P, N], F32, name="prod")
+            if m < MT - 1:
+                a_sb = left(m, e)
+                multiply(prod[:], right(m, e), a_sb[:])
+                for wm, wprod in waiting:
+                    add_into(nc.vector, wm, wprod[:])
+                waiting = []
+                add_into(nc.gpsimd, m, prod[:])
+                store(m)
+            else:
+                a_sb = left(m, e, parts=2)
+                half = N // 2
+                for lo in (0, half):
+                    multiply(prod[:, lo : lo + half], right(m, e, lo, lo + half), a_sb[:, lo : lo + half])
+                for lo in (0, half):
+                    add_into(nc.vector, m, prod[:, lo : lo + half], lo, lo + half)
+                    store(m, lo, lo + half)

@@ -22,7 +22,7 @@ K_PASS = P * PACK
 G = K // K_PASS
 MT = M // P
 V_ROW = 4
-WARMUP = 4
+WARMUP = 5
 LIN_PIECE = 128
 
 
@@ -45,8 +45,10 @@ def tile_volterra_quadratic_equaliser_s10_kernel(tc, x, u_words, u_scales, v_wor
         bias_row = kept([P, N], BF16, "bias_row")
         bias_all = kept([P, N], F32, "bias_all")
         ident = kept([P, P], F32, "ident")
-        u_plane = kept([P, G, R * N], U8, "u_plane")
-        v_plane = kept([P, G, R * N], U8, "v_plane")
+        u_first = kept([P, G, N], U8, "u_first")
+        v_first = kept([P, G, N], U8, "v_first")
+        uv_rest = kept([P, G, (R - 1) * N], U8, "uv_rest")
+        x_sorted = [kept([P, K // 2], F32, "x_sorted%d" % m) for m in range(MT // 2)]
         x_raw = [kept([P, K], BF16, "x_raw%d" % m) for m in range(2)]
         x_pair = [kept([P, 2, K], BF16, "x_pair%d" % j) for j in range(3)]
         x_codes = [kept([P, G * P], U32, "x_codes%d" % m) for m in range(MT)]
@@ -64,10 +66,11 @@ def tile_volterra_quadratic_equaliser_s10_kernel(tc, x, u_words, u_scales, v_wor
                 return x_raw[m][:]
             return x_pair[m // 2 - 1][:, m % 2, :]
 
-        nc.vector.memset(ones[:], 1.0)
-        nc.vector.memset(u_plane[:].rearrange("p g n -> p (g n)").bitcast(I32), 0)
-        nc.vector.memset(v_plane[:].rearrange("p g n -> p (g n)").bitcast(I32), 0)
+        nc.gpsimd.memset(ones[:], 1.0)
+        for plane in (u_first, v_first):
+            nc.vector.memset(plane[:].rearrange("p g n -> p (g n)").bitcast(I32), 0)
         nc.vector.memset(bias_row[:], 0.0)
+        nc.vector.memset(uv_rest[:].rearrange("p g n -> p (g n)").bitcast(I32), 0)
         make_identity(nc, ident[:])
 
         u_src = u_words.rearrange("g p b -> p g b")
@@ -81,9 +84,19 @@ def tile_volterra_quadratic_equaliser_s10_kernel(tc, x, u_words, u_scales, v_wor
         def load_v(e):
             nc.sync.dma_start(out=v_codes[e][:].bitcast(I32), in_=v_src[:, :, 4 * N * e : 4 * N * (e + 1)].bitcast(I32))
 
-        def load_scales(plane, src, row):
-            for q in range(4):
-                nc.sync.dma_start(out=plane[32 * q + row : 32 * q + row + 4, :, :].bitcast(I32), in_=src[4 * q : 4 * q + 4, :, :].bitcast(I32))
+        def load_scales(plane, src, row, lo, hi):
+            for r in range(4):
+                nc.sync.dma_start(out=plane[row + r : P : 32, :, :].bitcast(I32), in_=src[r:16:4, :, lo:hi].bitcast(I32))
+
+        def u_scale(e, g):
+            if e == 0:
+                return u_first[:, g, :]
+            return uv_rest[:, g, N * (e - 1) : N * e]
+
+        def v_scale(e, g, lo, hi):
+            if e == 0:
+                return v_first[V_ROW:P, g, lo:hi]
+            return uv_rest[V_ROW:P, g, N * (e - 1) + lo : N * (e - 1) + hi]
 
         def load_x_pair(j):
             rows = x[2 * P * (j + 1) : 2 * P * (j + 2), :]
@@ -91,23 +104,31 @@ def tile_volterra_quadratic_equaliser_s10_kernel(tc, x, u_words, u_scales, v_wor
 
         for m in range(2):
             nc.sync.dma_start(out=x_raw[m][:], in_=x[P * m : P * (m + 1), :])
-        load_u(0)
-        load_scales(u_plane, us_src, 0)
-        load_v(0)
-        nc.sync.dma_start(out=bias_row[0:1, :], in_=bias.rearrange("(o n) -> o n", o=1))
         load_x_pair(0)
-        load_scales(v_plane, vs_src, V_ROW)
+        load_u(0)
+        load_scales(u_first, us_src, 0, 0, N)
+        load_v(0)
+        load_scales(v_first, vs_src, V_ROW, 0, N)
         load_x_pair(1)
         load_x_pair(2)
+        nc.sync.dma_start(out=bias_row[0:1, :], in_=bias.rearrange("(o n) -> o n", o=1))
         load_u(1)
         load_v(1)
         for g in range(G):
             nc.sync.dma_start(out=lin_raw[g][:], in_=lin[K_PASS * g : K_PASS * (g + 1), :].rearrange("(p j) n -> p j n", j=PACK))
+        load_scales(uv_rest, us_src, 0, N, R * N)
+        load_scales(uv_rest, vs_src, V_ROW, N, R * N)
         for e in range(2, R):
             load_u(e)
             load_v(e)
 
         x_grouped = {}
+
+        def sort_x(m):
+            nc.vector.tensor_copy(
+                out=x_sorted[m - MT // 2][:].rearrange("p (g h c i) -> p g c h i", g=G, h=2, i=4),
+                in_=x_rows(m).bitcast(F32).rearrange("p (g c i h) -> p g c h i", g=G, h=2, i=4),
+            )
 
         def turn_x(m):
             words = x_rows(m).bitcast(F32)
@@ -115,7 +136,11 @@ def tile_volterra_quadratic_equaliser_s10_kernel(tc, x, u_words, u_scales, v_wor
             for g in range(G):
                 for h in range(2):
                     col = P * (2 * g + h)
-                    nc.tensor.transpose(bank[:, col : col + P], words[:, 2 * P * g + h : 2 * P * (g + 1) : 2], ident[:])
+                    if m < MT // 2:
+                        src = words[:, 2 * P * g + h : 2 * P * (g + 1) : 2]
+                    else:
+                        src = x_sorted[m - MT // 2][:, col : col + P]
+                    nc.tensor.transpose(bank[:, col : col + P], src, ident[:])
             grouped = stage.tile([P, G * P * PACK], BF16, name="x_grouped", align_bytes=256)
             nc.scalar.copy(
                 out=grouped[:].bitcast(F32).rearrange("p (g r h) -> p g r h", g=G, h=2),
@@ -140,8 +165,8 @@ def tile_volterra_quadratic_equaliser_s10_kernel(tc, x, u_words, u_scales, v_wor
 
         def left(m, e, parts=1):
             bank = new_bank()
-            passes(bank[:], m, lambda g: u_codes[e][:, g, :].bitcast(FP4X4), lambda g: u_plane[:, g, N * e : N * (e + 1)])
-            a_sb = stage.tile([P, N], F32, name="a_sb")
+            passes(bank[:], m, lambda g: u_codes[e][:, g, :].bitcast(FP4X4), lambda g: u_scale(e, g))
+            a_sb = stage.tile([P, N], F32, name="a_sb", bufs=6)
             w = N // parts
             for j in range(parts):
                 nc.scalar.copy(out=a_sb[:, w * j : w * (j + 1)], in_=bank[:, w * j : w * (j + 1)])
@@ -153,7 +178,7 @@ def tile_volterra_quadratic_equaliser_s10_kernel(tc, x, u_words, u_scales, v_wor
                 bank[:, 0 : hi - lo],
                 m,
                 lambda g: v_codes[e][:, g, lo:hi].bitcast(FP8X4),
-                lambda g: v_plane[V_ROW:P, g, N * e + lo : N * e + hi],
+                lambda g: v_scale(e, g, lo, hi),
             )
             return bank[:, 0 : hi - lo]
 
@@ -171,11 +196,13 @@ def tile_volterra_quadratic_equaliser_s10_kernel(tc, x, u_words, u_scales, v_wor
                 in_=lin_raw[g][:, :, cols].rearrange("p t (c i) -> p c t i", i=4),
             )
 
-        def quantize_lin(g):
+        def quantize_lin(part):
+            g, c = divmod(part, 2)
+            cols = slice(N // 2 * c, N // 2 * (c + 1))
             nc.vector.quantize_mx(
-                out=lin_codes[g][:].bitcast(FP8X4),
-                scales=lin_plane[g][:],
-                in_=lin_grouped[g][:].rearrange("p n t -> p (n t)"),
+                out=lin_codes[g][:, cols].bitcast(FP8X4),
+                scales=lin_plane[g][:, cols],
+                in_=lin_grouped[g][:, cols, :].rearrange("p n t -> p (n t)"),
             )
 
         def store(m, lo=0, hi=N):
@@ -185,54 +212,51 @@ def tile_volterra_quadratic_equaliser_s10_kernel(tc, x, u_words, u_scales, v_wor
         for i in range(WARMUP):
             nc.tensor.matmul(warm[:], lhsT=ones[:, 0:P], rhs=ones[:], start=True, stop=True)
 
-        turn_x(0)
-        turn_x(1)
-        quantize_x(0)
-        quantize_x(1)
+        half_m = MT // 2
+        for m in range(half_m):
+            turn_x(m)
+            quantize_x(m)
+        first = [left(m, 0) for m in range(half_m)]
+        sort_x(4)
+        sort_x(5)
+        multiply(acc[0][:], right(0, 0), first[0][:])
+        sort_x(6)
+        sort_x(7)
+        multiply(acc[1][:], right(1, 0), first[1][:])
         bias_bank = new_bank()
         nc.tensor.matmul(bias_bank[:], lhsT=ones[:, 0:P], rhs=bias_row[:], start=True, stop=True)
-        a0 = left(0, 0)
-        a1 = left(1, 0)
         nc.scalar.copy(out=bias_all[:], in_=bias_bank[:])
-        turn_x(2)
-        turn_x(3)
-        quantize_x(2)
-        quantize_x(3)
-        for m, a_sb in ((0, a0), (1, a1)):
-            multiply(acc[m][:], right(m, 0), a_sb[:])
-            add_into(nc.gpsimd, m, bias_all[:])
-        for m in range(2, MT):
-            if m < 4:
-                turn_x(2 * m)
-                turn_x(2 * m + 1)
-            a_sb = left(m, 0)
-            if m < 4:
-                quantize_x(2 * m)
-                quantize_x(2 * m + 1)
-            elif m % 2 == 0:
-                group_lin(m // 2 - 2)
-            multiply(acc[m][:], right(m, 0), a_sb[:])
-            add_into(nc.gpsimd, m, bias_all[:])
+        for m in range(half_m, MT):
+            turn_x(m)
+        add_into(nc.vector, 0, bias_all[:])
+        quantize_x(4)
+        add_into(nc.vector, 1, bias_all[:])
+        quantize_x(5)
+        quantize_x(6)
 
         waiting = []
-        for i in range(2 * MT):
-            e, m = 1 + i // MT, i % MT
-            a_sb = left(m, e)
-            if i % 2 == 0 and i // 2 + 2 < G * N // LIN_PIECE:
-                group_lin(i // 2 + 2)
-            prod = stage.tile([P, N], F32, name="prod")
-            multiply(prod[:], right(m, e), a_sb[:])
-            if i % 2 == 0:
-                for wm, wprod in waiting:
-                    add_into(nc.vector, wm, wprod[:])
-                waiting = []
-                add_into(nc.gpsimd, m, prod[:])
+        for i in range(2, 3 * MT):
+            e, m = divmod(i, MT)
+            a_sb = first[m] if i < half_m else left(m, e)
+            if i % 2 == 0 and 6 <= i <= 20:
+                group_lin(i // 2 - 3)
+            if e == 0:
+                multiply(acc[m][:], right(m, e), a_sb[:])
+                term = bias_all
             else:
-                waiting = [(m, prod)]
-            if i == 5:
-                quantize_lin(0)
-            if i == 13:
-                quantize_lin(1)
+                term = stage.tile([P, N], F32, name="prod")
+                multiply(term[:], right(m, e), a_sb[:])
+            if i == 2:
+                quantize_x(7)
+            if i % 2 == 0:
+                for wm, wterm in waiting:
+                    add_into(nc.vector, wm, wterm[:])
+                waiting = []
+                if i % 4 == 2 and i >= 10:
+                    quantize_lin(i // 4 - 2)
+                add_into(nc.gpsimd, m, term[:])
+            else:
+                waiting = [(m, term)]
 
         e = R - 1
         for m in range(MT):

@@ -22,7 +22,8 @@ K_PASS = P * PACK
 G = K // K_PASS
 MT = M // P
 V_ROW = 4
-WARMUP = 5
+WARMUP = 4
+HEAD = 3
 LIN_PIECE = 128
 
 
@@ -48,9 +49,9 @@ def tile_volterra_quadratic_equaliser_s10_kernel(tc, x, u_words, u_scales, v_wor
         u_first = kept([P, G, N], U8, "u_first")
         v_first = kept([P, G, N], U8, "v_first")
         uv_rest = kept([P, G, (R - 1) * N], U8, "uv_rest")
-        x_sorted = [kept([P, K // 2], F32, "x_sorted%d" % m) for m in range(MT // 2)]
-        x_raw = [kept([P, K], BF16, "x_raw%d" % m) for m in range(2)]
-        x_pair = [kept([P, 2, K], BF16, "x_pair%d" % j) for j in range(3)]
+        x_sorted = [kept([P, K // 2], F32, "x_sorted%d" % m) for m in range(MT - HEAD)]
+        x_raw = [kept([P, K], BF16, "x_raw%d" % m) for m in range(4)]
+        x_pair = [kept([P, 2, K], BF16, "x_pair%d" % j) for j in range(2)]
         x_codes = [kept([P, G * P], U32, "x_codes%d" % m) for m in range(MT)]
         x_plane = [kept([P, G * P], U8, "x_plane%d" % m) for m in range(MT)]
         u_codes = [kept([P, G, 2 * N], U8, "u_codes%d" % e) for e in range(R)]
@@ -62,14 +63,14 @@ def tile_volterra_quadratic_equaliser_s10_kernel(tc, x, u_words, u_scales, v_wor
         acc = [kept([P, N], F32, "acc%d" % m) for m in range(MT)]
 
         def x_rows(m):
-            if m < 2:
+            if m < 4:
                 return x_raw[m][:]
-            return x_pair[m // 2 - 1][:, m % 2, :]
+            return x_pair[m // 2 - 2][:, m % 2, :]
 
+        nc.gpsimd.memset(u_first[:].rearrange("p g n -> p (g n)").bitcast(I32), 0)
         nc.gpsimd.memset(ones[:], 1.0)
-        for plane in (u_first, v_first):
-            nc.vector.memset(plane[:].rearrange("p g n -> p (g n)").bitcast(I32), 0)
-        nc.vector.memset(bias_row[:], 0.0)
+        nc.vector.memset(v_first[:].rearrange("p g n -> p (g n)").bitcast(I32), 0)
+        nc.vector.memset(bias_row[:].bitcast(I32), 0)
         nc.vector.memset(uv_rest[:].rearrange("p g n -> p (g n)").bitcast(I32), 0)
         make_identity(nc, ident[:])
 
@@ -84,9 +85,9 @@ def tile_volterra_quadratic_equaliser_s10_kernel(tc, x, u_words, u_scales, v_wor
         def load_v(e):
             nc.sync.dma_start(out=v_codes[e][:].bitcast(I32), in_=v_src[:, :, 4 * N * e : 4 * N * (e + 1)].bitcast(I32))
 
-        def load_scales(plane, src, row, lo, hi):
+        def load_scales(queue, plane, src, row, lo, hi):
             for r in range(4):
-                nc.sync.dma_start(out=plane[row + r : P : 32, :, :].bitcast(I32), in_=src[r:16:4, :, lo:hi].bitcast(I32))
+                queue.dma_start(out=plane[row + r : P : 32, :, :].bitcast(I32), in_=src[r:16:4, :, lo:hi].bitcast(I32))
 
         def u_scale(e, g):
             if e == 0:
@@ -99,34 +100,42 @@ def tile_volterra_quadratic_equaliser_s10_kernel(tc, x, u_words, u_scales, v_wor
             return uv_rest[V_ROW:P, g, N * (e - 1) + lo : N * (e - 1) + hi]
 
         def load_x_pair(j):
-            rows = x[2 * P * (j + 1) : 2 * P * (j + 2), :]
+            rows = x[2 * P * (j + 2) : 2 * P * (j + 3), :]
             nc.sync.dma_start(out=x_pair[j][:], in_=rows.rearrange("(h p) k -> p h k", p=P))
 
-        for m in range(2):
+        def load_x(m):
             nc.sync.dma_start(out=x_raw[m][:], in_=x[P * m : P * (m + 1), :])
-        load_x_pair(0)
+
+        def load_lin(g):
+            nc.sync.dma_start(out=lin_raw[g][:], in_=lin[K_PASS * g : K_PASS * (g + 1), :].rearrange("(p j) n -> p j n", j=PACK))
+
+        load_x(0)
+        load_x(1)
+        load_scales(nc.sync, u_first, us_src, 0, 0, N)
+        load_x(2)
         load_u(0)
-        load_scales(u_first, us_src, 0, 0, N)
         load_v(0)
-        load_scales(v_first, vs_src, V_ROW, 0, N)
+        load_scales(nc.sync, v_first, vs_src, V_ROW, 0, N)
+        load_x(3)
+        load_x_pair(0)
         load_x_pair(1)
-        load_x_pair(2)
         nc.sync.dma_start(out=bias_row[0:1, :], in_=bias.rearrange("(o n) -> o n", o=1))
         load_u(1)
         load_v(1)
-        for g in range(G):
-            nc.sync.dma_start(out=lin_raw[g][:], in_=lin[K_PASS * g : K_PASS * (g + 1), :].rearrange("(p j) n -> p j n", j=PACK))
-        load_scales(uv_rest, us_src, 0, N, R * N)
-        load_scales(uv_rest, vs_src, V_ROW, N, R * N)
+        load_lin(0)
+        load_scales(nc.sync, uv_rest, us_src, 0, N, R * N)
+        load_scales(nc.sync, uv_rest, vs_src, V_ROW, N, R * N)
+        load_lin(1)
         for e in range(2, R):
             load_u(e)
             load_v(e)
 
         x_grouped = {}
+        x_banks = {}
 
-        def sort_x(m):
-            nc.vector.tensor_copy(
-                out=x_sorted[m - MT // 2][:].rearrange("p (g h c i) -> p g c h i", g=G, h=2, i=4),
+        def sort_x(copy, m):
+            copy(
+                out=x_sorted[m - HEAD][:].rearrange("p (g h c i) -> p g c h i", g=G, h=2, i=4),
                 in_=x_rows(m).bitcast(F32).rearrange("p (g c i h) -> p g c h i", g=G, h=2, i=4),
             )
 
@@ -136,11 +145,15 @@ def tile_volterra_quadratic_equaliser_s10_kernel(tc, x, u_words, u_scales, v_wor
             for g in range(G):
                 for h in range(2):
                     col = P * (2 * g + h)
-                    if m < MT // 2:
+                    if m < HEAD:
                         src = words[:, 2 * P * g + h : 2 * P * (g + 1) : 2]
                     else:
-                        src = x_sorted[m - MT // 2][:, col : col + P]
+                        src = x_sorted[m - HEAD][:, col : col + P]
                     nc.tensor.transpose(bank[:, col : col + P], src, ident[:])
+            x_banks[m] = bank
+
+        def group_x(m):
+            bank = x_banks[m]
             grouped = stage.tile([P, G * P * PACK], BF16, name="x_grouped", align_bytes=256)
             nc.scalar.copy(
                 out=grouped[:].bitcast(F32).rearrange("p (g r h) -> p g r h", g=G, h=2),
@@ -163,13 +176,25 @@ def tile_volterra_quadratic_equaliser_s10_kernel(tc, x, u_words, u_scales, v_wor
                     stop=(g == G - 1),
                 )
 
-        def left(m, e, parts=1):
+        def left(m, e):
             bank = new_bank()
             passes(bank[:], m, lambda g: u_codes[e][:, g, :].bitcast(FP4X4), lambda g: u_scale(e, g))
             a_sb = stage.tile([P, N], F32, name="a_sb", bufs=6)
-            w = N // parts
-            for j in range(parts):
-                nc.scalar.copy(out=a_sb[:, w * j : w * (j + 1)], in_=bank[:, w * j : w * (j + 1)])
+            nc.scalar.copy(out=a_sb[:], in_=bank[:])
+            return a_sb
+
+        def left_in_halves(m, e):
+            a_sb = stage.tile([P, N], F32, name="a_sb", bufs=6)
+            for lo in (0, N // 2):
+                bank = new_bank()
+                for c in (lo, lo + P):
+                    passes(
+                        bank[:, c - lo : c - lo + P],
+                        m,
+                        lambda g: u_codes[e][:, g, 2 * c : 2 * (c + P)].bitcast(FP4X4),
+                        lambda g: u_scale(e, g)[:, c : c + P],
+                    )
+                nc.scalar.copy(out=a_sb[:, lo : lo + N // 2], in_=bank[:, 0 : N // 2])
             return a_sb
 
         def right(m, e, lo=0, hi=N):
@@ -208,72 +233,87 @@ def tile_volterra_quadratic_equaliser_s10_kernel(tc, x, u_words, u_scales, v_wor
         def store(m, lo=0, hi=N):
             nc.sync.dma_start(out=out[P * m : P * (m + 1), lo:hi], in_=acc[m][:, lo:hi])
 
-        warm = new_bank()
-        for i in range(WARMUP):
-            nc.tensor.matmul(warm[:], lhsT=ones[:, 0:P], rhs=ones[:], start=True, stop=True)
+        def warm_up(count):
+            warm = new_bank()
+            for i in range(count):
+                nc.tensor.matmul(warm[:], lhsT=ones[:, 0:P], rhs=ones[:], start=True, stop=True)
 
-        half_m = MT // 2
-        for m in range(half_m):
+        warm_up(WARMUP)
+
+        for m in range(HEAD):
             turn_x(m)
+            group_x(m)
             quantize_x(m)
-        first = [left(m, 0) for m in range(half_m)]
-        sort_x(4)
-        sort_x(5)
-        multiply(acc[0][:], right(0, 0), first[0][:])
-        sort_x(6)
-        sort_x(7)
-        multiply(acc[1][:], right(1, 0), first[1][:])
+        first = [left(m, 0) for m in range(HEAD)]
+        for m in range(HEAD):
+            sort_x(nc.scalar.copy, HEAD + m)
+            multiply(acc[m][:], right(m, 0), first[m][:])
         bias_bank = new_bank()
         nc.tensor.matmul(bias_bank[:], lhsT=ones[:, 0:P], rhs=bias_row[:], start=True, stop=True)
         nc.scalar.copy(out=bias_all[:], in_=bias_bank[:])
-        for m in range(half_m, MT):
+        for m in range(2 * HEAD, MT):
+            sort_x(nc.vector.tensor_copy, m)
+        for m in range(HEAD, MT):
             turn_x(m)
-        add_into(nc.vector, 0, bias_all[:])
-        quantize_x(4)
-        add_into(nc.vector, 1, bias_all[:])
-        quantize_x(5)
-        quantize_x(6)
+        for m in range(HEAD, 2 * HEAD):
+            group_x(m)
+            quantize_x(m)
+            if m == HEAD:
+                add_into(nc.vector, 1, bias_all[:])
 
-        waiting = []
-        for i in range(2, 3 * MT):
+        waiting = [(0, bias_all), (2, bias_all)]
+        for i in range(HEAD, 3 * MT):
             e, m = divmod(i, MT)
-            a_sb = first[m] if i < half_m else left(m, e)
-            if i % 2 == 0 and 6 <= i <= 20:
-                group_lin(i // 2 - 3)
+            a_sb = left(m, e)
+            if i == HEAD:
+                group_x(6)
+                group_x(7)
+            if i % 2 == 1 and 5 <= i <= 19:
+                group_lin(i // 2 - 2)
             if e == 0:
                 multiply(acc[m][:], right(m, e), a_sb[:])
                 term = bias_all
             else:
                 term = stage.tile([P, N], F32, name="prod")
                 multiply(term[:], right(m, e), a_sb[:])
-            if i == 2:
-                quantize_x(7)
-            if i % 2 == 0:
+            if i in (3, 4):
+                quantize_x(i + 3)
+            if i % 2 == 1:
                 for wm, wterm in waiting:
                     add_into(nc.vector, wm, wterm[:])
                 waiting = []
-                if i % 4 == 2 and i >= 10:
+                if i % 4 == 1 and i >= 9:
                     quantize_lin(i // 4 - 2)
                 add_into(nc.gpsimd, m, term[:])
             else:
                 waiting = [(m, term)]
 
         e = R - 1
-        for m in range(MT):
+        def add_linear(m):
             d_bank = new_bank()
             passes(d_bank[:], m, lambda g: lin_codes[g][:].bitcast(FP8X4), lambda g: lin_plane[g][:])
             nc.vector.tensor_tensor(out=acc[m][:], in0=d_bank[:], in1=acc[m][:], op=ADD)
+
+        late = MT - 3
+        for m in range(MT):
+            if m < late:
+                add_linear(m)
+            elif m == late:
+                add_linear(m + 1)
+            elif m == MT - 1:
+                add_linear(m)
+                add_linear(late)
+                store(late)
+                store(late + 1)
             prod = stage.tile([P, N], F32, name="prod")
             if m < MT - 1:
                 a_sb = left(m, e)
                 multiply(prod[:], right(m, e), a_sb[:])
-                for wm, wprod in waiting:
-                    add_into(nc.vector, wm, wprod[:])
-                waiting = []
                 add_into(nc.gpsimd, m, prod[:])
-                store(m)
+                if m < late:
+                    store(m)
             else:
-                a_sb = left(m, e, parts=2)
+                a_sb = left_in_halves(m, e)
                 half = N // 2
                 for lo in (0, half):
                     multiply(prod[:, lo : lo + half], right(m, e, lo, lo + half), a_sb[:, lo : lo + half])

@@ -60,7 +60,8 @@ def tile_volterra_quadratic_equaliser_s10_kernel(tc, x, u_words, u_scales, v_wor
         lin_grouped = [kept([P, N, PACK], BF16, "lin_grouped%d" % g) for g in range(G)]
         lin_codes = [kept([P, N], U32, "lin_codes%d" % g) for g in range(G)]
         lin_plane = [kept([P, N], U8, "lin_plane%d" % g) for g in range(G)]
-        acc = [kept([P, N], F32, "acc%d" % m) for m in range(MT)]
+        acc_two = [kept([P, 2, N], F32, "acc_two%d" % j) for j in range(MT // 2)]
+        acc = [acc_two[m // 2][:, m % 2, :] for m in range(MT)]
 
         def x_rows(m):
             if m < 4:
@@ -116,10 +117,10 @@ def tile_volterra_quadratic_equaliser_s10_kernel(tc, x, u_words, u_scales, v_wor
         load_u(0)
         load_v(0)
         load_scales(nc.sync, v_first, vs_src, V_ROW, 0, N)
+        nc.sync.dma_start(out=bias_row[0:1, :], in_=bias.rearrange("(o n) -> o n", o=1))
         load_x(3)
         load_x_pair(0)
         load_x_pair(1)
-        nc.sync.dma_start(out=bias_row[0:1, :], in_=bias.rearrange("(o n) -> o n", o=1))
         load_u(1)
         load_v(1)
         load_lin(0)
@@ -213,6 +214,9 @@ def tile_volterra_quadratic_equaliser_s10_kernel(tc, x, u_words, u_scales, v_wor
         def add_into(engine, m, term, lo=0, hi=N):
             engine.tensor_tensor(out=acc[m][:, lo:hi], in0=acc[m][:, lo:hi], in1=term, op=ADD)
 
+        def add_two(engine, j, terms):
+            engine.tensor_tensor(out=acc_two[j][:], in0=acc_two[j][:], in1=terms, op=ADD)
+
         def group_lin(piece):
             g, c = divmod(piece, N // LIN_PIECE)
             cols = slice(LIN_PIECE * c, LIN_PIECE * (c + 1))
@@ -247,7 +251,7 @@ def tile_volterra_quadratic_equaliser_s10_kernel(tc, x, u_words, u_scales, v_wor
         first = [left(m, 0) for m in range(HEAD)]
         for m in range(HEAD):
             sort_x(nc.scalar.copy, HEAD + m)
-            multiply(acc[m][:], right(m, 0), first[m][:])
+            multiply(acc[m], right(m, 0), first[m][:])
         bias_bank = new_bank()
         nc.tensor.matmul(bias_bank[:], lhsT=ones[:, 0:P], rhs=bias_row[:], start=True, stop=True)
         nc.scalar.copy(out=bias_all[:], in_=bias_bank[:])
@@ -258,10 +262,11 @@ def tile_volterra_quadratic_equaliser_s10_kernel(tc, x, u_words, u_scales, v_wor
         for m in range(HEAD, 2 * HEAD):
             group_x(m)
             quantize_x(m)
-            if m == HEAD:
-                add_into(nc.vector, 1, bias_all[:])
+            if m % 2 == 1:
+                add_into(nc.vector, m // 2 - 1, bias_all[:])
 
-        waiting = [(0, bias_all), (2, bias_all)]
+        waiting = None
+        terms = bias_all[:].unsqueeze(1).to_broadcast([P, 2, N])
         for i in range(HEAD, 3 * MT):
             e, m = divmod(i, MT)
             a_sb = left(m, e)
@@ -271,28 +276,28 @@ def tile_volterra_quadratic_equaliser_s10_kernel(tc, x, u_words, u_scales, v_wor
             if i % 2 == 1 and 5 <= i <= 19:
                 group_lin(i // 2 - 2)
             if e == 0:
-                multiply(acc[m][:], right(m, e), a_sb[:])
-                term = bias_all
+                multiply(acc[m], right(m, e), a_sb[:])
             else:
-                term = stage.tile([P, N], F32, name="prod")
-                multiply(term[:], right(m, e), a_sb[:])
-            if i in (3, 4):
-                quantize_x(i + 3)
-            if i % 2 == 1:
-                for wm, wterm in waiting:
-                    add_into(nc.vector, wm, wterm[:])
-                waiting = []
-                if i % 4 == 1 and i >= 9:
+                if m % 2 == 0:
+                    prod_two = stage.tile([P, 2, N], F32, name="prod_two")
+                    terms = prod_two[:]
+                multiply(terms[:, m % 2, :], right(m, e), a_sb[:])
+            if i == HEAD:
+                quantize_x(6)
+                quantize_x(7)
+            if i % 4 == 1:
+                add_two(nc.vector, *waiting)
+                if i >= 9:
                     quantize_lin(i // 4 - 2)
-                add_into(nc.gpsimd, m, term[:])
-            else:
-                waiting = [(m, term)]
+                add_two(nc.gpsimd, m // 2, terms)
+            elif i % 4 == 3:
+                waiting = (m // 2, terms)
 
         e = R - 1
         def add_linear(m):
             d_bank = new_bank()
             passes(d_bank[:], m, lambda g: lin_codes[g][:].bitcast(FP8X4), lambda g: lin_plane[g][:])
-            nc.vector.tensor_tensor(out=acc[m][:], in0=d_bank[:], in1=acc[m][:], op=ADD)
+            nc.vector.tensor_tensor(out=acc[m], in0=d_bank[:], in1=acc[m], op=ADD)
 
         late = MT - 3
         for m in range(MT):
@@ -309,6 +314,8 @@ def tile_volterra_quadratic_equaliser_s10_kernel(tc, x, u_words, u_scales, v_wor
             if m < MT - 1:
                 a_sb = left(m, e)
                 multiply(prod[:], right(m, e), a_sb[:])
+                if m == 0:
+                    add_two(nc.vector, *waiting)
                 add_into(nc.gpsimd, m, prod[:])
                 if m < late:
                     store(m)

@@ -21,10 +21,18 @@ PACK = 4
 K_PASS = P * PACK
 G = K // K_PASS
 MT = M // P
+HALF = N // 2
 V_ROW = 4
 WARMUP = 4
 HEAD = 3
+SINGLE = 4
 LIN_PIECE = 128
+LIN_PIECES = G * N // LIN_PIECE
+LIN_START = 5
+STAGE_BUFS = 4
+LEFT_BUFS = 6
+PSUM_BANKS = 8
+ALIGN = 256
 
 
 def tile_volterra_quadratic_equaliser_s10_kernel(tc, x, u_words, u_scales, v_words, v_scales, lin, bias, out):
@@ -32,12 +40,12 @@ def tile_volterra_quadratic_equaliser_s10_kernel(tc, x, u_words, u_scales, v_wor
 
     with ExitStack() as ctx:
         keep = ctx.enter_context(tc.tile_pool(name="keep", bufs=1))
-        stage = ctx.enter_context(tc.tile_pool(name="stage", bufs=4))
-        psum = ctx.enter_context(tc.psum_pool(name="psum", bufs=8))
+        stage = ctx.enter_context(tc.tile_pool(name="stage", bufs=STAGE_BUFS))
+        psum = ctx.enter_context(tc.psum_pool(name="psum", bufs=PSUM_BANKS))
         ctx.enter_context(tc.manual_schedule())
 
         def kept(shape, dtype, name):
-            return keep.tile(shape, dtype, name=name, align_bytes=256)
+            return keep.tile(shape, dtype, name=name, align_bytes=ALIGN)
 
         def new_bank():
             return psum.tile([P, N], F32, name="bank", tag="bank")
@@ -50,8 +58,8 @@ def tile_volterra_quadratic_equaliser_s10_kernel(tc, x, u_words, u_scales, v_wor
         v_first = kept([P, G, N], U8, "v_first")
         uv_rest = kept([P, G, (R - 1) * N], U8, "uv_rest")
         x_sorted = [kept([P, K // 2], F32, "x_sorted%d" % m) for m in range(MT - HEAD)]
-        x_raw = [kept([P, K], BF16, "x_raw%d" % m) for m in range(4)]
-        x_pair = [kept([P, 2, K], BF16, "x_pair%d" % j) for j in range(2)]
+        x_raw = [kept([P, K], BF16, "x_raw%d" % m) for m in range(SINGLE)]
+        x_pair = [kept([P, 2, K], BF16, "x_pair%d" % j) for j in range((MT - SINGLE) // 2)]
         x_codes = [kept([P, G * P], U32, "x_codes%d" % m) for m in range(MT)]
         x_plane = [kept([P, G * P], U8, "x_plane%d" % m) for m in range(MT)]
         u_codes = [kept([P, G, 2 * N], U8, "u_codes%d" % e) for e in range(R)]
@@ -64,9 +72,9 @@ def tile_volterra_quadratic_equaliser_s10_kernel(tc, x, u_words, u_scales, v_wor
         acc = [acc_two[m // 2][:, m % 2, :] for m in range(MT)]
 
         def x_rows(m):
-            if m < 4:
+            if m < SINGLE:
                 return x_raw[m][:]
-            return x_pair[m // 2 - 2][:, m % 2, :]
+            return x_pair[(m - SINGLE) // 2][:, m % 2, :]
 
         nc.gpsimd.memset(u_first[:].rearrange("p g n -> p (g n)").bitcast(I32), 0)
         nc.gpsimd.memset(ones[:], 1.0)
@@ -86,9 +94,40 @@ def tile_volterra_quadratic_equaliser_s10_kernel(tc, x, u_words, u_scales, v_wor
         def load_v(e):
             nc.sync.dma_start(out=v_codes[e][:].bitcast(I32), in_=v_src[:, :, 4 * N * e : 4 * N * (e + 1)].bitcast(I32))
 
-        def load_scales(queue, plane, src, row, lo, hi):
+        def load_scales(plane, src, row, lo, hi):
             for r in range(4):
-                queue.dma_start(out=plane[row + r : P : 32, :, :].bitcast(I32), in_=src[r:16:4, :, lo:hi].bitcast(I32))
+                nc.sync.dma_start(out=plane[row + r : P : 32, :, :].bitcast(I32), in_=src[r:16:4, :, lo:hi].bitcast(I32))
+
+        def load_x(m):
+            nc.sync.dma_start(out=x_raw[m][:], in_=x[P * m : P * (m + 1), :])
+
+        def load_x_pair(j):
+            rows = x[P * (SINGLE + 2 * j) : P * (SINGLE + 2 * j + 2), :]
+            nc.sync.dma_start(out=x_pair[j][:], in_=rows.rearrange("(h p) k -> p h k", p=P))
+
+        def load_lin(g):
+            nc.sync.dma_start(out=lin_raw[g][:], in_=lin[K_PASS * g : K_PASS * (g + 1), :].rearrange("(p j) n -> p j n", j=PACK))
+
+        load_x(0)
+        load_x(1)
+        load_scales(u_first, us_src, 0, 0, N)
+        load_x(2)
+        load_u(0)
+        load_v(0)
+        load_scales(v_first, vs_src, V_ROW, 0, N)
+        nc.sync.dma_start(out=bias_row[0:1, :], in_=bias.rearrange("(o n) -> o n", o=1))
+        load_x(3)
+        load_x_pair(0)
+        load_x_pair(1)
+        load_u(1)
+        load_v(1)
+        load_lin(0)
+        load_scales(uv_rest, us_src, 0, N, R * N)
+        load_scales(uv_rest, vs_src, V_ROW, N, R * N)
+        load_lin(1)
+        for e in range(2, R):
+            load_u(e)
+            load_v(e)
 
         def u_scale(e, g):
             if e == 0:
@@ -100,37 +139,6 @@ def tile_volterra_quadratic_equaliser_s10_kernel(tc, x, u_words, u_scales, v_wor
                 return v_first[V_ROW:P, g, lo:hi]
             return uv_rest[V_ROW:P, g, N * (e - 1) + lo : N * (e - 1) + hi]
 
-        def load_x_pair(j):
-            rows = x[2 * P * (j + 2) : 2 * P * (j + 3), :]
-            nc.sync.dma_start(out=x_pair[j][:], in_=rows.rearrange("(h p) k -> p h k", p=P))
-
-        def load_x(m):
-            nc.sync.dma_start(out=x_raw[m][:], in_=x[P * m : P * (m + 1), :])
-
-        def load_lin(g):
-            nc.sync.dma_start(out=lin_raw[g][:], in_=lin[K_PASS * g : K_PASS * (g + 1), :].rearrange("(p j) n -> p j n", j=PACK))
-
-        load_x(0)
-        load_x(1)
-        load_scales(nc.sync, u_first, us_src, 0, 0, N)
-        load_x(2)
-        load_u(0)
-        load_v(0)
-        load_scales(nc.sync, v_first, vs_src, V_ROW, 0, N)
-        nc.sync.dma_start(out=bias_row[0:1, :], in_=bias.rearrange("(o n) -> o n", o=1))
-        load_x(3)
-        load_x_pair(0)
-        load_x_pair(1)
-        load_u(1)
-        load_v(1)
-        load_lin(0)
-        load_scales(nc.sync, uv_rest, us_src, 0, N, R * N)
-        load_scales(nc.sync, uv_rest, vs_src, V_ROW, N, R * N)
-        load_lin(1)
-        for e in range(2, R):
-            load_u(e)
-            load_v(e)
-
         x_grouped = {}
         x_banks = {}
 
@@ -141,29 +149,45 @@ def tile_volterra_quadratic_equaliser_s10_kernel(tc, x, u_words, u_scales, v_wor
             )
 
         def turn_x(m):
-            words = x_rows(m).bitcast(F32)
+            pairs = x_rows(m).bitcast(F32)
             bank = new_bank()
             for g in range(G):
                 for h in range(2):
                     col = P * (2 * g + h)
                     if m < HEAD:
-                        src = words[:, 2 * P * g + h : 2 * P * (g + 1) : 2]
+                        src = pairs[:, 2 * P * g + h : 2 * P * (g + 1) : 2]
                     else:
                         src = x_sorted[m - HEAD][:, col : col + P]
                     nc.tensor.transpose(bank[:, col : col + P], src, ident[:])
             x_banks[m] = bank
 
         def group_x(m):
-            bank = x_banks[m]
-            grouped = stage.tile([P, G * P * PACK], BF16, name="x_grouped", align_bytes=256)
+            grouped = stage.tile([P, G * P * PACK], BF16, name="x_grouped", align_bytes=ALIGN)
             nc.scalar.copy(
                 out=grouped[:].bitcast(F32).rearrange("p (g r h) -> p g r h", g=G, h=2),
-                in_=bank[:].rearrange("p (g h r) -> p g r h", g=G, h=2),
+                in_=x_banks[m][:].rearrange("p (g h r) -> p g r h", g=G, h=2),
             )
             x_grouped[m] = grouped
 
         def quantize_x(m):
             nc.vector.quantize_mx(out=x_codes[m][:].bitcast(FP8X4), scales=x_plane[m][:], in_=x_grouped[m][:])
+
+        def group_lin(piece):
+            g, c = divmod(piece, N // LIN_PIECE)
+            cols = slice(LIN_PIECE * c, LIN_PIECE * (c + 1))
+            nc.scalar.copy(
+                out=lin_grouped[g][:, cols, :].rearrange("p (c i) t -> p c t i", i=4),
+                in_=lin_raw[g][:, :, cols].rearrange("p t (c i) -> p c t i", i=4),
+            )
+
+        def quantize_lin(part):
+            g, c = divmod(part, 2)
+            cols = slice(HALF * c, HALF * (c + 1))
+            nc.vector.quantize_mx(
+                out=lin_codes[g][:, cols].bitcast(FP8X4),
+                scales=lin_plane[g][:, cols],
+                in_=lin_grouped[g][:, cols, :].rearrange("p n t -> p (n t)"),
+            )
 
         def passes(bank_cols, m, rhs_of, scale_of):
             for g in range(G):
@@ -180,13 +204,13 @@ def tile_volterra_quadratic_equaliser_s10_kernel(tc, x, u_words, u_scales, v_wor
         def left(m, e):
             bank = new_bank()
             passes(bank[:], m, lambda g: u_codes[e][:, g, :].bitcast(FP4X4), lambda g: u_scale(e, g))
-            a_sb = stage.tile([P, N], F32, name="a_sb", bufs=6)
+            a_sb = stage.tile([P, N], F32, name="a_sb", bufs=LEFT_BUFS)
             nc.scalar.copy(out=a_sb[:], in_=bank[:])
             return a_sb
 
         def left_in_halves(m, e):
-            a_sb = stage.tile([P, N], F32, name="a_sb", bufs=6)
-            for lo in (0, N // 2):
+            a_sb = stage.tile([P, N], F32, name="a_sb", bufs=LEFT_BUFS)
+            for lo in (0, HALF):
                 bank = new_bank()
                 for c in (lo, lo + P):
                     passes(
@@ -195,7 +219,7 @@ def tile_volterra_quadratic_equaliser_s10_kernel(tc, x, u_words, u_scales, v_wor
                         lambda g: u_codes[e][:, g, 2 * c : 2 * (c + P)].bitcast(FP4X4),
                         lambda g: u_scale(e, g)[:, c : c + P],
                     )
-                nc.scalar.copy(out=a_sb[:, lo : lo + N // 2], in_=bank[:, 0 : N // 2])
+                nc.scalar.copy(out=a_sb[:, lo : lo + HALF], in_=bank[:, 0:HALF])
             return a_sb
 
         def right(m, e, lo=0, hi=N):
@@ -217,64 +241,53 @@ def tile_volterra_quadratic_equaliser_s10_kernel(tc, x, u_words, u_scales, v_wor
         def add_two(engine, j, terms):
             engine.tensor_tensor(out=acc_two[j][:], in0=acc_two[j][:], in1=terms, op=ADD)
 
-        def group_lin(piece):
-            g, c = divmod(piece, N // LIN_PIECE)
-            cols = slice(LIN_PIECE * c, LIN_PIECE * (c + 1))
-            nc.scalar.copy(
-                out=lin_grouped[g][:, cols, :].rearrange("p (c i) t -> p c t i", i=4),
-                in_=lin_raw[g][:, :, cols].rearrange("p t (c i) -> p c t i", i=4),
-            )
-
-        def quantize_lin(part):
-            g, c = divmod(part, 2)
-            cols = slice(N // 2 * c, N // 2 * (c + 1))
-            nc.vector.quantize_mx(
-                out=lin_codes[g][:, cols].bitcast(FP8X4),
-                scales=lin_plane[g][:, cols],
-                in_=lin_grouped[g][:, cols, :].rearrange("p n t -> p (n t)"),
-            )
+        def add_linear(m):
+            d_bank = new_bank()
+            passes(d_bank[:], m, lambda g: lin_codes[g][:].bitcast(FP8X4), lambda g: lin_plane[g][:])
+            nc.vector.tensor_tensor(out=acc[m], in0=d_bank[:], in1=acc[m], op=ADD)
 
         def store(m, lo=0, hi=N):
             nc.sync.dma_start(out=out[P * m : P * (m + 1), lo:hi], in_=acc[m][:, lo:hi])
 
-        def warm_up(count):
-            warm = new_bank()
-            for i in range(count):
-                nc.tensor.matmul(warm[:], lhsT=ones[:, 0:P], rhs=ones[:], start=True, stop=True)
-
-        warm_up(WARMUP)
+        warm = new_bank()
+        for i in range(WARMUP):
+            nc.tensor.matmul(warm[:], lhsT=ones[:, 0:P], rhs=ones[:], start=True, stop=True)
 
         for m in range(HEAD):
             turn_x(m)
             group_x(m)
             quantize_x(m)
         first = [left(m, 0) for m in range(HEAD)]
-        for m in range(HEAD):
-            sort_x(nc.scalar.copy, HEAD + m)
+        second_run = range(HEAD, HEAD + 2)
+        third_run = range(HEAD + 2, MT)
+        for m in range(HEAD - 1):
+            sort_x(nc.scalar.copy, second_run[m])
             multiply(acc[m], right(m, 0), first[m][:])
+        for m in third_run:
+            sort_x(nc.vector.tensor_copy, m)
         bias_bank = new_bank()
         nc.tensor.matmul(bias_bank[:], lhsT=ones[:, 0:P], rhs=bias_row[:], start=True, stop=True)
-        nc.scalar.copy(out=bias_all[:], in_=bias_bank[:])
-        for m in range(2 * HEAD, MT):
-            sort_x(nc.vector.tensor_copy, m)
-        for m in range(HEAD, MT):
+        for m in second_run:
             turn_x(m)
-        for m in range(HEAD, 2 * HEAD):
             group_x(m)
             quantize_x(m)
-            if m % 2 == 1:
-                add_into(nc.vector, m // 2 - 1, bias_all[:])
+        nc.scalar.copy(out=bias_all[:], in_=bias_bank[:])
+        multiply(acc[HEAD - 1], right(HEAD - 1, 0), first[HEAD - 1][:])
+        for j, m in enumerate(third_run):
+            turn_x(m)
+            group_x(m)
+            if j < 2:
+                add_into(nc.vector, j, bias_all[:])
+            quantize_x(m)
 
-        waiting = None
+        vector_pair = None
         terms = bias_all[:].unsqueeze(1).to_broadcast([P, 2, N])
-        for i in range(HEAD, 3 * MT):
+        for i in range(HEAD, (R - 1) * MT):
             e, m = divmod(i, MT)
             a_sb = left(m, e)
-            if i == HEAD:
-                group_x(6)
-                group_x(7)
-            if i % 2 == 1 and 5 <= i <= 19:
-                group_lin(i // 2 - 2)
+            lin_piece, odd = divmod(i - LIN_START, 2)
+            if 0 <= lin_piece < LIN_PIECES and not odd:
+                group_lin(lin_piece)
             if e == 0:
                 multiply(acc[m], right(m, e), a_sb[:])
             else:
@@ -282,23 +295,15 @@ def tile_volterra_quadratic_equaliser_s10_kernel(tc, x, u_words, u_scales, v_wor
                     prod_two = stage.tile([P, 2, N], F32, name="prod_two")
                     terms = prod_two[:]
                 multiply(terms[:, m % 2, :], right(m, e), a_sb[:])
-            if i == HEAD:
-                quantize_x(6)
-                quantize_x(7)
-            if i % 4 == 1:
-                add_two(nc.vector, *waiting)
-                if i >= 9:
-                    quantize_lin(i // 4 - 2)
+            if m % 4 == 1:
+                add_two(nc.vector, *vector_pair)
+                if lin_piece >= 2:
+                    quantize_lin(lin_piece // 2 - 1)
                 add_two(nc.gpsimd, m // 2, terms)
-            elif i % 4 == 3:
-                waiting = (m // 2, terms)
+            elif m % 4 == 3:
+                vector_pair = (m // 2, terms)
 
         e = R - 1
-        def add_linear(m):
-            d_bank = new_bank()
-            passes(d_bank[:], m, lambda g: lin_codes[g][:].bitcast(FP8X4), lambda g: lin_plane[g][:])
-            nc.vector.tensor_tensor(out=acc[m], in0=d_bank[:], in1=acc[m], op=ADD)
-
         late = MT - 3
         for m in range(MT):
             if m < late:
@@ -315,15 +320,14 @@ def tile_volterra_quadratic_equaliser_s10_kernel(tc, x, u_words, u_scales, v_wor
                 a_sb = left(m, e)
                 multiply(prod[:], right(m, e), a_sb[:])
                 if m == 0:
-                    add_two(nc.vector, *waiting)
+                    add_two(nc.vector, *vector_pair)
                 add_into(nc.gpsimd, m, prod[:])
                 if m < late:
                     store(m)
             else:
                 a_sb = left_in_halves(m, e)
-                half = N // 2
-                for lo in (0, half):
-                    multiply(prod[:, lo : lo + half], right(m, e, lo, lo + half), a_sb[:, lo : lo + half])
-                for lo in (0, half):
-                    add_into(nc.vector, m, prod[:, lo : lo + half], lo, lo + half)
-                    store(m, lo, lo + half)
+                for lo in (0, HALF):
+                    multiply(prod[:, lo : lo + HALF], right(m, e, lo, lo + HALF), a_sb[:, lo : lo + HALF])
+                for lo in (0, HALF):
+                    add_into(nc.vector, m, prod[:, lo : lo + HALF], lo, lo + HALF)
+                    store(m, lo, lo + HALF)

from contextlib import ExitStack

import concourse.mybir as mybir
from concourse.masks import make_identity

M, K, N, R = 1024, 1024, 512, 4
FLOPS = 2 * M * K * (2 * R * N + N) + 2 * M * R * N + M * N

F32 = mybir.dt.float32
BF16 = mybir.dt.bfloat16
I32 = mybir.dt.int32
U32 = mybir.dt.uint32
U8 = mybir.dt.uint8
FP8X4 = mybir.dt.float8_e4m3fn_x4
FP4X4 = mybir.dt.float4_e2m1fn_x4
ADD = mybir.AluOpType.add
MULT = mybir.AluOpType.mult

P = 128
PACK = 4
K_PASS = P * PACK
G = K // K_PASS
MT = M // P
HALF = N // 2
V_ROW = 4
WARMUP = 4
HEAD = 3
SINGLE = 4
LIN_PIECE = 128
LIN_PIECES = G * N // LIN_PIECE
LIN_START = 5
STAGE_BUFS = 4
LEFT_BUFS = 6
PSUM_BANKS = 8
ALIGN = 256


def tile_volterra_quadratic_equaliser_s10_kernel(tc, x, u_words, u_scales, v_words, v_scales, lin, bias, out):
    nc = tc.nc

    with ExitStack() as ctx:
        keep = ctx.enter_context(tc.tile_pool(name="keep", bufs=1))
        stage = ctx.enter_context(tc.tile_pool(name="stage", bufs=STAGE_BUFS))
        psum = ctx.enter_context(tc.psum_pool(name="psum", bufs=PSUM_BANKS))
        ctx.enter_context(tc.manual_schedule())

        def kept(shape, dtype, name):
            return keep.tile(shape, dtype, name=name, align_bytes=ALIGN)

        def new_bank():
            return psum.tile([P, N], F32, name="bank", tag="bank")

        ones = kept([P, N], BF16, "ones")
        bias_row = kept([P, N], BF16, "bias_row")
        bias_all = kept([P, N], F32, "bias_all")
        ident = kept([P, P], F32, "ident")
        u_first = kept([P, G, N], U8, "u_first")
        v_first = kept([P, G, N], U8, "v_first")
        uv_rest = kept([P, G, (R - 1) * N], U8, "uv_rest")
        x_sorted = [kept([P, K // 2], F32, "x_sorted%d" % m) for m in range(MT - HEAD)]
        x_raw = [kept([P, K], BF16, "x_raw%d" % m) for m in range(SINGLE)]
        x_pair = [kept([P, 2, K], BF16, "x_pair%d" % j) for j in range((MT - SINGLE) // 2)]
        x_codes = [kept([P, G * P], U32, "x_codes%d" % m) for m in range(MT)]
        x_plane = [kept([P, G * P], U8, "x_plane%d" % m) for m in range(MT)]
        u_codes = [kept([P, G, 2 * N], U8, "u_codes%d" % e) for e in range(R)]
        v_codes = [kept([P, G, N], U32, "v_codes%d" % e) for e in range(R)]
        lin_raw = [kept([P, PACK, N], BF16, "lin_raw%d" % g) for g in range(G)]
        lin_grouped = [kept([P, N, PACK], BF16, "lin_grouped%d" % g) for g in range(G)]
        lin_codes = [kept([P, N], U32, "lin_codes%d" % g) for g in range(G)]
        lin_plane = [kept([P, N], U8, "lin_plane%d" % g) for g in range(G)]
        acc_two = [kept([P, 2, N], F32, "acc_two%d" % j) for j in range(MT // 2)]
        acc = [acc_two[m // 2][:, m % 2, :] for m in range(MT)]

        def x_rows(m):
            if m < SINGLE:
                return x_raw[m][:]
            return x_pair[(m - SINGLE) // 2][:, m % 2, :]

        nc.gpsimd.memset(u_first[:].rearrange("p g n -> p (g n)").bitcast(I32), 0)
        nc.gpsimd.memset(ones[:], 1.0)
        nc.vector.memset(v_first[:].rearrange("p g n -> p (g n)").bitcast(I32), 0)
        nc.vector.memset(bias_row[:].bitcast(I32), 0)
        nc.vector.memset(uv_rest[:].rearrange("p g n -> p (g n)").bitcast(I32), 0)
        make_identity(nc, ident[:])

        u_src = u_words.rearrange("g p b -> p g b")
        v_src = v_words.rearrange("g p n t -> p g (n t)")
        us_src = u_scales.rearrange("g q n -> q g n")
        vs_src = v_scales.rearrange("g q n -> q g n")

        def load_u(e):
            nc.sync.dma_start(out=u_codes[e][:].bitcast(I32), in_=u_src[:, :, 2 * N * e : 2 * N * (e + 1)].bitcast(I32))

        def load_v(e):
            nc.sync.dma_start(out=v_codes[e][:].bitcast(I32), in_=v_src[:, :, 4 * N * e : 4 * N * (e + 1)].bitcast(I32))

        def load_scales(plane, src, row, lo, hi):
            for r in range(4):
                nc.sync.dma_start(out=plane[row + r : P : 32, :, :].bitcast(I32), in_=src[r:16:4, :, lo:hi].bitcast(I32))

        def load_x(m):
            nc.sync.dma_start(out=x_raw[m][:], in_=x[P * m : P * (m + 1), :])

        def load_x_pair(j):
            rows = x[P * (SINGLE + 2 * j) : P * (SINGLE + 2 * j + 2), :]
            nc.sync.dma_start(out=x_pair[j][:], in_=rows.rearrange("(h p) k -> p h k", p=P))

        def load_lin(g):
            nc.sync.dma_start(out=lin_raw[g][:], in_=lin[K_PASS * g : K_PASS * (g + 1), :].rearrange("(p j) n -> p j n", j=PACK))

        load_x(0)
        load_x(1)
        load_scales(u_first, us_src, 0, 0, N)
        load_x(2)
        load_u(0)
        load_v(0)
        load_scales(v_first, vs_src, V_ROW, 0, N)
        nc.sync.dma_start(out=bias_row[0:1, :], in_=bias.rearrange("(o n) -> o n", o=1))
        load_x(3)
        load_x_pair(0)
        load_x_pair(1)
        load_u(1)
        load_v(1)
        load_lin(0)
        load_scales(uv_rest, us_src, 0, N, R * N)
        load_scales(uv_rest, vs_src, V_ROW, N, R * N)
        load_lin(1)
        for e in range(2, R):
            load_u(e)
            load_v(e)

        def u_scale(e, g):
            if e == 0:
                return u_first[:, g, :]
            return uv_rest[:, g, N * (e - 1) : N * e]

        def v_scale(e, g, lo, hi):
            if e == 0:
                return v_first[V_ROW:P, g, lo:hi]
            return uv_rest[V_ROW:P, g, N * (e - 1) + lo : N * (e - 1) + hi]

        x_grouped = {}
        x_banks = {}

        def sort_x(copy, m):
            copy(
                out=x_sorted[m - HEAD][:].rearrange("p (g h c i) -> p g c h i", g=G, h=2, i=4),
                in_=x_rows(m).bitcast(F32).rearrange("p (g c i h) -> p g c h i", g=G, h=2, i=4),
            )

        def turn_x(m):
            pairs = x_rows(m).bitcast(F32)
            bank = new_bank()
            for g in range(G):
                for h in range(2):
                    col = P * (2 * g + h)
                    if m < HEAD:
                        src = pairs[:, 2 * P * g + h : 2 * P * (g + 1) : 2]
                    else:
                        src = x_sorted[m - HEAD][:, col : col + P]
                    nc.tensor.transpose(bank[:, col : col + P], src, ident[:])
            x_banks[m] = bank

        def group_x(m):
            grouped = stage.tile([P, G * P * PACK], BF16, name="x_grouped", align_bytes=ALIGN)
            nc.scalar.copy(
                out=grouped[:].bitcast(F32).rearrange("p (g r h) -> p g r h", g=G, h=2),
                in_=x_banks[m][:].rearrange("p (g h r) -> p g r h", g=G, h=2),
            )
            x_grouped[m] = grouped

        def quantize_x(m):
            nc.vector.quantize_mx(out=x_codes[m][:].bitcast(FP8X4), scales=x_plane[m][:], in_=x_grouped[m][:])

        def group_lin(piece):
            g, c = divmod(piece, N // LIN_PIECE)
            cols = slice(LIN_PIECE * c, LIN_PIECE * (c + 1))
            nc.scalar.copy(
                out=lin_grouped[g][:, cols, :].rearrange("p (c i) t -> p c t i", i=4),
                in_=lin_raw[g][:, :, cols].rearrange("p t (c i) -> p c t i", i=4),
            )

        def quantize_lin(part):
            g, c = divmod(part, 2)
            cols = slice(HALF * c, HALF * (c + 1))
            nc.vector.quantize_mx(
                out=lin_codes[g][:, cols].bitcast(FP8X4),
                scales=lin_plane[g][:, cols],
                in_=lin_grouped[g][:, cols, :].rearrange("p n t -> p (n t)"),
            )

        def passes(bank_cols, m, rhs_of, scale_of):
            for g in range(G):
                nc.tensor.matmul_mx(
                    out=bank_cols,
                    lhsT=x_codes[m][:, P * g : P * (g + 1)].bitcast(FP8X4),
                    lhsT_scale=x_plane[m][:, P * g : P * (g + 1)],
                    rhs=rhs_of(g),
                    rhs_scale=scale_of(g),
                    start=(g == 0),
                    stop=(g == G - 1),
                )

        def left(m, e):
            bank = new_bank()
            passes(bank[:], m, lambda g: u_codes[e][:, g, :].bitcast(FP4X4), lambda g: u_scale(e, g))
            a_sb = stage.tile([P, N], F32, name="a_sb", bufs=LEFT_BUFS)
            nc.scalar.copy(out=a_sb[:], in_=bank[:])
            return a_sb

        def left_in_halves(m, e):
            a_sb = stage.tile([P, N], F32, name="a_sb", bufs=LEFT_BUFS)
            for lo in (0, HALF):
                bank = new_bank()
                for c in (lo, lo + P):
                    passes(
                        bank[:, c - lo : c - lo + P],
                        m,
                        lambda g: u_codes[e][:, g, 2 * c : 2 * (c + P)].bitcast(FP4X4),
                        lambda g: u_scale(e, g)[:, c : c + P],
                    )
                nc.scalar.copy(out=a_sb[:, lo : lo + HALF], in_=bank[:, 0:HALF])
            return a_sb

        def right(m, e, lo=0, hi=N):
            bank = new_bank()
            passes(
                bank[:, 0 : hi - lo],
                m,
                lambda g: v_codes[e][:, g, lo:hi].bitcast(FP8X4),
                lambda g: v_scale(e, g, lo, hi),
            )
            return bank[:, 0 : hi - lo]

        def multiply(dst, c_bank, a_sb):
            nc.vector.tensor_tensor(out=dst, in0=c_bank, in1=a_sb, op=MULT)

        def add_into(engine, m, term, lo=0, hi=N):
            engine.tensor_tensor(out=acc[m][:, lo:hi], in0=acc[m][:, lo:hi], in1=term, op=ADD)

        def add_two(engine, j, terms):
            engine.tensor_tensor(out=acc_two[j][:], in0=acc_two[j][:], in1=terms, op=ADD)

        def add_linear(m):
            d_bank = new_bank()
            passes(d_bank[:], m, lambda g: lin_codes[g][:].bitcast(FP8X4), lambda g: lin_plane[g][:])
            nc.vector.tensor_tensor(out=acc[m], in0=d_bank[:], in1=acc[m], op=ADD)

        def store(m, lo=0, hi=N):
            nc.sync.dma_start(out=out[P * m : P * (m + 1), lo:hi], in_=acc[m][:, lo:hi])

        warm = new_bank()
        for i in range(WARMUP):
            nc.tensor.matmul(warm[:], lhsT=ones[:, 0:P], rhs=ones[:], start=True, stop=True)

        for m in range(HEAD):
            turn_x(m)
            group_x(m)
            quantize_x(m)
        first = [left(m, 0) for m in range(HEAD)]
        second_run = range(HEAD, HEAD + 2)
        third_run = range(HEAD + 2, MT)
        for m in range(HEAD - 1):
            sort_x(nc.scalar.copy, second_run[m])
            multiply(acc[m], right(m, 0), first[m][:])
        for m in third_run:
            sort_x(nc.vector.tensor_copy, m)
        bias_bank = new_bank()
        nc.tensor.matmul(bias_bank[:], lhsT=ones[:, 0:P], rhs=bias_row[:], start=True, stop=True)
        for m in second_run:
            turn_x(m)
            group_x(m)
            quantize_x(m)
        nc.scalar.copy(out=bias_all[:], in_=bias_bank[:])
        multiply(acc[HEAD - 1], right(HEAD - 1, 0), first[HEAD - 1][:])
        for j, m in enumerate(third_run):
            turn_x(m)
            group_x(m)
            if j < 2:
                add_into(nc.vector, j, bias_all[:])
            quantize_x(m)

        vector_pair = None
        terms = bias_all[:].unsqueeze(1).to_broadcast([P, 2, N])
        for i in range(HEAD, (R - 1) * MT):
            e, m = divmod(i, MT)
            a_sb = left(m, e)
            lin_piece, odd = divmod(i - LIN_START, 2)
            if 0 <= lin_piece < LIN_PIECES and not odd:
                group_lin(lin_piece)
            if e == 0:
                multiply(acc[m], right(m, e), a_sb[:])
            else:
                if m % 2 == 0:
                    prod_two = stage.tile([P, 2, N], F32, name="prod_two")
                    terms = prod_two[:]
                multiply(terms[:, m % 2, :], right(m, e), a_sb[:])
            if m % 4 == 1:
                add_two(nc.vector, *vector_pair)
                if lin_piece >= 2:
                    quantize_lin(lin_piece // 2 - 1)
                add_two(nc.gpsimd, m // 2, terms)
            elif m % 4 == 3:
                vector_pair = (m // 2, terms)

        e = R - 1
        late = MT - 3
        for m in range(MT):
            if m < late:
                add_linear(m)
            elif m == late:
                add_linear(m + 1)
            elif m == MT - 1:
                add_linear(m)
                add_linear(late)
                store(late)
                store(late + 1)
            prod = stage.tile([P, N], F32, name="prod")
            if m < MT - 1:
                a_sb = left(m, e)
                multiply(prod[:], right(m, e), a_sb[:])
                if m == 0:
                    add_two(nc.vector, *vector_pair)
                add_into(nc.gpsimd, m, prod[:])
                if m < late:
                    store(m)
            else:
                a_sb = left_in_halves(m, e)
                for lo in (0, HALF):
                    multiply(prod[:, lo : lo + HALF], right(m, e, lo, lo + HALF), a_sb[:, lo : lo + HALF])
                for lo in (0, HALF):
                    add_into(nc.vector, m, prod[:, lo : lo + HALF], lo, lo + HALF)
                    store(m, lo, lo + HALF)
